import numpy as np
import ml_dtypes


def mxq(x, axis, fmt="e4m3"):
    dtype, down = {"e4m3": (ml_dtypes.float8_e4m3fn, 7), "e5m2": (ml_dtypes.float8_e5m2, 14)}[fmt]
    v = np.moveaxis(np.asarray(x, np.float32).astype(ml_dtypes.bfloat16).astype(np.float64), axis, -1)
    blocks = v.reshape(v.shape[:-1] + (-1, 32))
    amax = np.abs(blocks).max(-1, keepdims=True)
    byte = np.maximum(np.where(amax > 0, np.frexp(amax)[1] - 1 + 127, 0) - down, 1)
    scale = np.exp2(byte - 127.0)
    codes = (blocks / scale).astype(np.float32).astype(dtype).astype(np.float64)
    return np.moveaxis((codes * scale).reshape(v.shape), -1, axis)


WIDE = False


def mx_kscale(k):
    if not WIDE:
        return np.ones(k)
    levels = np.array([10, -10, 5, -5, 0])
    if k % 512:
        return np.exp2(np.random.permutation(np.resize(levels, k // 32))).repeat(32)
    a = np.empty((k // 512, 16))
    for p in range(k // 512):
        a[p, :8] = np.random.permutation(np.resize(levels, 8))
        for g in range(8):
            far = levels[np.abs(levels - a[p, g]) >= 10]
            a[p, g + 8] = far[np.random.randint(len(far))]
    return np.exp2(a.ravel()).repeat(32)


def f64(x):
    return np.asarray(x).astype(np.float64)


def striped(idx):
    return np.tile(idx.reshape(-1, 16).T, (8, 1)).astype(np.uint16)


def unstriped(offs):
    return offs[:16].T.reshape(-1).astype(np.int64)


def pack_weight(w):
    k, n = w.shape
    w = f64(np.asarray(w, np.float32).astype(ml_dtypes.bfloat16)).reshape(k // 32, 32, n)
    amax = np.abs(w).max(1)
    byte = np.clip(np.where(amax > 0, np.frexp(amax)[1] - 1 + 127 - 7, 1), 1, 254)
    scaled = (w * np.exp2(127.0 - byte)[:, None, :]).reshape(k, n).astype(np.float32)
    words = np.ascontiguousarray(scaled.reshape(k // 512, 128, 4, n).transpose(0, 1, 3, 2)).astype(ml_dtypes.float8_e4m3fn).view(np.uint8)
    return words, np.ascontiguousarray(byte.astype(np.uint8).reshape(k // 512, 16, n))


def unpack_weight(words, scales):
    g, p, n, _ = words.shape
    vals = np.ascontiguousarray(words).view(ml_dtypes.float8_e4m3fn).astype(np.float64) * np.repeat(np.exp2(scales.astype(np.float64) - 127.0), 8, axis=1)[..., None]
    return vals.transpose(0, 1, 3, 2).reshape(g * 512, n)


K, T, S, N, H, V = 1024, 2048, 512, 128, 512, 256


def setup_inputs():
    n = np.random.standard_normal
    s = mx_kscale(K)[:, None]
    u = mx_kscale(H)
    packed_xT = pack_weight(n((K, T)) * s)
    return {
        "x_words": packed_xT[0],
        "x_scales": packed_xT[1],
        "w1": (n((K, H)) / np.sqrt(K) / s).astype(np.float32),
        "t1": (1.2 * n((H, S))).astype(np.float32),
        "unit": (np.random.uniform(0.6, 1.4, (H, 1)) * u[:, None]).astype(np.float32),
        "w2": (n((H, N)) / np.sqrt(H) / u[:, None]).astype(np.float32),
        "offs": striped(np.random.permutation(T)[:S]),
        "qtr": striped(np.random.permutation(S)[:V]),
        "lag": striped(np.random.permutation(S)[:V]),
    }


def reference(x_words, x_scales, w1, t1, unit, w2, offs, qtr, lag):
    xq = unpack_weight(x_words, x_scales)[:, unstriped(offs)]
    y = mxq(f64(w1), 0, "e4m3").T @ xq
    we1 = np.exp(0.8 * (np.tanh(f64(t1))))
    we2 = np.exp(-0.8 * (np.tanh(1.7 * f64(t1))))
    den = we1 + we2 + 1.0
    mid = (y + we1 * (np.pad(y, ((0, 0), (0, 1)))[:, 1:]) + we2 * (np.pad(y, ((0, 0), (0, 2)))[:, 2:])) / den
    zq = mid[:, unstriped(qtr)]
    zl = mid[:, unstriped(lag)]
    gr = zq - (0.7 * zl)
    hid = f64(unit) * (gr * (np.exp(-1.0 * ((y[:, unstriped(lag)]) ** 2))))
    return mxq(f64(w2), 0, "e4m3").T @ mxq(hid, 0, "e4m3")

@@ -1,0 +1,229 @@
+from contextlib import ExitStack
+
+import concourse.mybir as mybir
+from concourse.masks import make_identity
+
+K, T, S, N, H, V = 1024, 2048, 512, 128, 512, 256
+FLOPS = 2 * K * H * S + 2 * H * N * V
+
+F32 = mybir.dt.float32
+BF16 = mybir.dt.bfloat16
+I32 = mybir.dt.int32
+U32 = mybir.dt.uint32
+U16 = mybir.dt.uint16
+U8 = mybir.dt.uint8
+FP8X4 = mybir.dt.float8_e4m3fn_x4
+ACT = mybir.ActivationFunctionType
+ALU = mybir.AluOpType
+
+P = 128
+PACK = 4
+PASSES = K // (P * PACK)
+W1_CHUNKS = (((0, 256), (256, 512)), ((0, 256), (256, 384), (384, 512)))
+VH = V // 2
+
+
+def tile_picked_yalmon_star_p_kernel(
+    tc, x_words, x_scales, w1, t1, unit, w2, offs, qtr, lag, out
+):
+    nc = tc.nc
+    with ExitStack() as ctx:
+        keep = ctx.enter_context(tc.tile_pool(name="keep", bufs=1))
+        psum = ctx.enter_context(tc.psum_pool(name="psum", bufs=1))
+
+        def tiles(name, count, shape, dtype):
+            return [keep.tile(shape, dtype, name="%s%d" % (name, i), tag="%s%d" % (name, i), align_bytes=64) for i in range(count)]
+
+        offs_sb = keep.tile([P, S // 16], U16, name="offs_sb")
+        qtr_sb = keep.tile([P, V // 16], U16, name="qtr_sb")
+        lag_sb = keep.tile([P, V // 16], U16, name="lag_sb")
+        unit_sb = keep.tile([P, PACK], F32, name="unit_sb")
+        t_sb = tiles("t_sb", PACK, [P, S], F32)
+        xw = tiles("xw", PASSES, [P, T], U32)
+        xs = keep.tile([P, T], U8, name="xs", align_bytes=64)
+        w1_raw = [
+            [keep.tile([P, PACK, hi - lo], F32, name="w1_raw%d_%d" % (o, lo), align_bytes=64) for lo, hi in W1_CHUNKS[o]]
+            for o in range(PASSES)
+        ]
+        w2_raw = keep.tile([P, PACK, N], F32, name="w2_raw", align_bytes=64)
+
+        nc.vector.memset(xs[:].bitcast(I32), 0)
+        shifted = tiles("shifted", PACK, [P, 2, S], F32)
+        for t in range(PACK):
+            nc.vector.memset(shifted[t][:, :, S - 2 :], 0.0)
+
+        t_rows = t1.rearrange("(p t) c -> p t c", t=PACK)
+        nc.sync.dma_start(out=t_sb[0][:], in_=t_rows[:, 0, :])
+        nc.sync.dma_start(out=t_sb[1][:], in_=t_rows[:, 1, :])
+        nc.sync.dma_start(offs_sb[:], offs)
+        for q in range(4):
+            nc.sync.dma_start(
+                out=xs[32 * q : 32 * q + 4 * PASSES, :].bitcast(I32),
+                in_=x_scales[:, 4 * q : 4 * q + 4, :].bitcast(I32),
+            )
+        nc.sync.dma_start(out=t_sb[2][:], in_=t_rows[:, 2, :])
+        nc.sync.dma_start(out=t_sb[3][:], in_=t_rows[:, 3, :])
+        for o in range(PASSES):
+            nc.sync.dma_start(out=xw[o][:].bitcast(I32), in_=x_words[o].rearrange("p n r -> p (n r)").bitcast(I32))
+        for o in range(PASSES):
+            rows = w1[512 * o : 512 * (o + 1), :].rearrange("(p j) c -> p j c", j=PACK)
+            for h, (lo, hi) in enumerate(W1_CHUNKS[o]):
+                nc.sync.dma_start(out=w1_raw[o][h][:], in_=rows[:, :, lo:hi])
+        nc.sync.dma_start(out=unit_sb[:], in_=unit.rearrange("(p t) o -> p (t o)", t=PACK))
+        nc.sync.dma_start(qtr_sb[:], qtr)
+        nc.sync.dma_start(lag_sb[:], lag)
+        nc.sync.dma_start(out=w2_raw[:], in_=w2.rearrange("(p j) c -> p j c", j=PACK))
+
+        th1 = tiles("th1", PACK, [P, S], F32)
+        th2 = tiles("th2", PACK, [P, S], F32)
+        we1 = tiles("we1", PACK, [P, S], F32)
+        we2 = tiles("we2", PACK, [P, S], F32)
+        ident = keep.tile([P, P], F32, name="ident", align_bytes=64)
+        make_identity(nc, ident[:])
+        lden = tiles("lden", PACK, [P, S], F32)
+        wsum = [psum.tile([P, S], F32, name="wsum%d" % t, tag="aux%d" % t) for t in range(PACK)]
+        for t in range(PACK):
+            nc.scalar.activation(th1[t][:], t_sb[t][:], ACT.Tanh)
+            nc.scalar.activation(th2[t][:], t_sb[t][:], ACT.Tanh, scale=1.7)
+            nc.scalar.activation(we1[t][:], th1[t][:], ACT.Exp, scale=0.8)
+            nc.scalar.activation(we2[t][:], th2[t][:], ACT.Exp, scale=-0.8)
+            for b in range(S // P):
+                cols = slice(P * b, P * (b + 1))
+                nc.tensor.matmul(wsum[t][:, cols], lhsT=we1[t][:, cols], rhs=ident[:], is_transpose=True, start=True, stop=False)
+                nc.tensor.matmul(wsum[t][:, cols], lhsT=we2[t][:, cols], rhs=ident[:], is_transpose=True, start=False, stop=True)
+        for t in range(PACK):
+            nc.scalar.activation(lden[t][:], wsum[t][:], ACT.Ln, bias=1.0)
+        gs = keep.tile([P, S], U8, name="gs", align_bytes=64)
+        gw = tiles("gw", PASSES, [P, S], U32)
+        nc.vector.tensor_copy(gs[:], xs[:].indirect(offs_sb[:]))
+        for o in range(PASSES):
+            nc.vector.tensor_copy(gw[o][:], xw[o][:].indirect(offs_sb[:]))
+
+        w1_bf = tiles("w1_bf", PASSES, [P, H * PACK], BF16)
+        w1_codes = tiles("w1_codes", PASSES, [P, H], U32)
+        w1_sc = tiles("w1_sc", PASSES, [P, H], U8)
+        ybank = [psum.tile([P, S], F32, name="ybank%d" % t) for t in range(PACK)]
+        for o in range(PASSES):
+            dst = w1_bf[o][:].rearrange("p (t m j) -> p m t j", t=PACK, j=PACK)
+            for h, (lo, hi) in enumerate(W1_CHUNKS[o]):
+                nc.vector.tensor_copy(
+                    dst[:, lo // PACK : hi // PACK, :, :],
+                    w1_raw[o][h][:].rearrange("p j (m t) -> p m t j", t=PACK),
+                )
+            for lo, hi in ((0, H),) if o == 0 else ((0, 128), (128, 256), (256, 512)):
+                nc.vector.quantize_mx(
+                    out=w1_codes[o][:, lo:hi].bitcast(FP8X4), scales=w1_sc[o][:, lo:hi], in_=w1_bf[o][:, PACK * lo : PACK * hi]
+                )
+            for t in range(PACK):
+                cols = slice(P * t, P * (t + 1))
+                nc.tensor.matmul_mx(
+                    out=ybank[t][:],
+                    lhsT=w1_codes[o][:, cols].bitcast(FP8X4),
+                    lhsT_scale=w1_sc[o][:, cols],
+                    rhs=gw[o][:].bitcast(FP8X4),
+                    rhs_scale=gs[4 * o :, :],
+                    start=(o == 0),
+                    stop=(o == PASSES - 1),
+                )
+
+        rden_t = keep.tile([P, PACK * S], F32, name="rden_t", tag="w1_bf1", align_bytes=64)
+        rden = [psum.tile([P, S], F32, name="rden%d" % t, tag="aux%d" % t) for t in range(PACK)]
+        for t in range(PACK):
+            nc.scalar.activation(rden_t[:, t * S : (t + 1) * S], lden[t][:], ACT.Exp, scale=-1.0)
+            for b in range(S // P):
+                nc.tensor.transpose(rden[t][:, P * b : P * (b + 1)], rden_t[:, t * S + P * b : t * S + P * (b + 1)], ident[:])
+
+        part = tiles("part", PACK, [P, S], F32)
+        num = tiles("num", PACK, [P, S], F32)
+        mid = tiles("mid", PACK, [P, S], F32)
+        ysq = tiles("ysq", PACK, [P, S], F32)
+        zq = tiles("zq", PACK, [P, V], F32)
+        zl = tiles("zl", PACK, [P, V], F32)
+        sl = tiles("sl", PACK, [P, V], F32)
+        damp = tiles("damp", PACK, [P, V], F32)
+        gr = tiles("gr", PACK, [P, V], F32)
+        hid = keep.tile([P, PACK, V], F32, name="hid", align_bytes=64)
+
+        def side(t):
+            return nc.vector if t == PACK - 1 else nc.gpsimd
+
+        def numerator(t):
+            y = ybank[t]
+            nc.vector.tensor_tensor(shifted[t][:, 0, : S - 1], y[:, 1:], we1[t][:, : S - 1], ALU.mult)
+            nc.vector.tensor_tensor(shifted[t][:, 1, : S - 2], y[:, 2:], we2[t][:, : S - 2], ALU.mult)
+            nc.vector.tensor_tensor(part[t][:], y[:], shifted[t][:, 0, :], ALU.add)
+            nc.gpsimd.tensor_tensor(num[t][:], part[t][:], shifted[t][:, 1, :], ALU.add)
+
+        def damping(t):
+            nc.scalar.activation(ysq[t][:], ybank[t][:], ACT.Square)
+            if t in ():
+                nc.vector.tensor_copy(sl[t][:], ysq[t][:].indirect(lag_sb[:]))
+            else:
+                nc.scalar.activation(sl[t][:], ysq[t][:].indirect(lag_sb[:]), ACT.Copy)
+            nc.scalar.activation(damp[t][:], sl[t][:], ACT.Exp, scale=-1.0)
+
+        def average(t):
+            nc.vector.scalar_tensor_tensor(mid[t][:], num[t][:], unit_sb[:, t : t + 1], rden[t][:], ALU.mult, ALU.mult)
+
+        def hidden(t):
+            width = VH if t == PACK - 1 else V
+            for lo in range(0, V, width):
+                cols = slice(lo, lo + width)
+                entries = slice(lo // 16, (lo + width) // 16)
+                if t in ():
+                    nc.scalar.activation(zq[t][:, cols], mid[t][:].indirect(qtr_sb[:, entries]), ACT.Copy)
+                else:
+                    nc.vector.tensor_copy(zq[t][:, cols], mid[t][:].indirect(qtr_sb[:, entries]))
+                nc.scalar.activation(zl[t][:, cols], mid[t][:].indirect(lag_sb[:, entries]), ACT.Copy, scale=-0.7)
+                side(t).tensor_tensor(gr[t][:, cols], zl[t][:, cols], zq[t][:, cols], ALU.add)
+                side(t).tensor_tensor(hid[:, t, cols], gr[t][:, cols], damp[t][:, cols], ALU.mult)
+
+        numerator(0)
+        numerator(1)
+        numerator(2)
+        average(0)
+        average(1)
+        damping(0)
+        hidden(0)
+        numerator(3)
+        average(2)
+        damping(1)
+        hidden(1)
+        average(3)
+        damping(2)
+        hidden(2)
+        damping(3)
+        hidden(3)
+
+        w2_bf = keep.tile([P, N * PACK], BF16, name="w2_bf", align_bytes=64)
+        w2_codes = keep.tile([P, N], U32, name="w2_codes", align_bytes=64)
+        w2_sc = keep.tile([P, N], U8, name="w2_sc", align_bytes=64)
+        nc.vector.tensor_copy(
+            w2_bf[:].rearrange("p (c i j) -> p c j i", i=4, j=PACK),
+            w2_raw[:].rearrange("p j (c i) -> p c j i", i=4),
+        )
+        nc.vector.quantize_mx(out=w2_codes[:].bitcast(FP8X4), scales=w2_sc[:], in_=w2_bf[:])
+
+        hid_bf = tiles("hid_bf", V // VH, [P, VH * PACK], BF16)
+        hid_codes = tiles("hid_codes", V // VH, [P, VH], U32)
+        hid_sc = tiles("hid_sc", V // VH, [P, VH], U8)
+        res = tiles("res", V // VH, [P, VH], F32)
+        for h in range(V // VH):
+            cols = slice(h * VH, (h + 1) * VH)
+            nc.vector.tensor_copy(
+                hid_bf[h][:].rearrange("p (c i t) -> p c t i", i=4, t=PACK),
+                hid[:, :, cols].rearrange("p t (c i) -> p c t i", i=4),
+            )
+            nc.vector.quantize_mx(out=hid_codes[h][:].bitcast(FP8X4), scales=hid_sc[h][:], in_=hid_bf[h][:])
+            obank = psum.tile([P, VH], F32, name="obank%d" % h, tag="aux%d" % h)
+            nc.tensor.matmul_mx(
+                out=obank[:],
+                lhsT=w2_codes[:].bitcast(FP8X4),
+                lhsT_scale=w2_sc[:],
+                rhs=hid_codes[h][:].bitcast(FP8X4),
+                rhs_scale=hid_sc[h][:],
+                start=True,
+                stop=True,
+            )
+            nc.scalar.copy(res[h][:], obank[:])
+            nc.sync.dma_start(out=out[:, cols], in_=res[h][:])

@@ -38,13 +38,12 @@ def tile_picked_yalmon_star_p_kernel(
         qtr_sb = keep.tile([P, V // 16], U16, name="qtr_sb")
         lag_sb = keep.tile([P, V // 16], U16, name="lag_sb")
         unit_sb = keep.tile([P, PACK], F32, name="unit_sb")
-        t_sb = tiles("t_sb", PACK, [P, S], F32)
+        t_first = keep.tile([P, S], F32, name="t_first", align_bytes=64)
+        t_rest = keep.tile([P, PACK - 1, S], F32, name="t_rest", align_bytes=64)
+        t_sb = [t_first[:]] + [t_rest[:, t, :] for t in range(PACK - 1)]
         xw = tiles("xw", PASSES, [P, T], U32)
         xs = keep.tile([P, T], U8, name="xs", align_bytes=64)
-        w1_raw = [
-            [keep.tile([P, PACK, hi - lo], F32, name="w1_raw%d_%d" % (o, lo), align_bytes=64) for lo, hi in W1_CHUNKS[o]]
-            for o in range(PASSES)
-        ]
+        w1_raw = tiles("w1_raw", PASSES, [P, PACK, H], F32)
         w2_raw = keep.tile([P, PACK, N], F32, name="w2_raw", align_bytes=64)
 
         nc.vector.memset(xs[:].bitcast(I32), 0)
@@ -53,22 +52,22 @@ def tile_picked_yalmon_star_p_kernel(
             nc.vector.memset(shifted[t][:, :, S - 2 :], 0.0)
 
         t_rows = t1.rearrange("(p t) c -> p t c", t=PACK)
-        nc.sync.dma_start(out=t_sb[0][:], in_=t_rows[:, 0, :])
-        nc.sync.dma_start(out=t_sb[1][:], in_=t_rows[:, 1, :])
+        nc.sync.dma_start(out=t_first[:], in_=t_rows[:, 0, :])
+        nc.sync.dma_start(out=t_rest[:], in_=t_rows[:, 1:, :])
         nc.sync.dma_start(offs_sb[:], offs)
         for q in range(4):
             nc.sync.dma_start(
                 out=xs[32 * q : 32 * q + 4 * PASSES, :].bitcast(I32),
                 in_=x_scales[:, 4 * q : 4 * q + 4, :].bitcast(I32),
             )
-        nc.sync.dma_start(out=t_sb[2][:], in_=t_rows[:, 2, :])
-        nc.sync.dma_start(out=t_sb[3][:], in_=t_rows[:, 3, :])
-        for o in range(PASSES):
+
+        def load_words(o):
             nc.sync.dma_start(out=xw[o][:].bitcast(I32), in_=x_words[o].rearrange("p n r -> p (n r)").bitcast(I32))
+
+        load_words(0)
         for o in range(PASSES):
-            rows = w1[512 * o : 512 * (o + 1), :].rearrange("(p j) c -> p j c", j=PACK)
-            for h, (lo, hi) in enumerate(W1_CHUNKS[o]):
-                nc.sync.dma_start(out=w1_raw[o][h][:], in_=rows[:, :, lo:hi])
+            nc.sync.dma_start(out=w1_raw[o][:], in_=w1[512 * o : 512 * (o + 1), :].rearrange("(p j) c -> p j c", j=PACK))
+        load_words(1)
         nc.sync.dma_start(out=unit_sb[:], in_=unit.rearrange("(p t) o -> p (t o)", t=PACK))
         nc.sync.dma_start(qtr_sb[:], qtr)
         nc.sync.dma_start(lag_sb[:], lag)
@@ -83,8 +82,8 @@ def tile_picked_yalmon_star_p_kernel(
         lden = tiles("lden", PACK, [P, S], F32)
         wsum = [psum.tile([P, S], F32, name="wsum%d" % t, tag="aux%d" % t) for t in range(PACK)]
         for t in range(PACK):
-            nc.scalar.activation(th1[t][:], t_sb[t][:], ACT.Tanh)
-            nc.scalar.activation(th2[t][:], t_sb[t][:], ACT.Tanh, scale=1.7)
+            nc.scalar.activation(th1[t][:], t_sb[t], ACT.Tanh)
+            nc.scalar.activation(th2[t][:], t_sb[t], ACT.Tanh, scale=1.7)
             nc.scalar.activation(we1[t][:], th1[t][:], ACT.Exp, scale=0.8)
             nc.scalar.activation(we2[t][:], th2[t][:], ACT.Exp, scale=-0.8)
             for b in range(S // P):
@@ -94,39 +93,42 @@ def tile_picked_yalmon_star_p_kernel(
         for t in range(PACK):
             nc.scalar.activation(lden[t][:], wsum[t][:], ACT.Ln, bias=1.0)
         gs = keep.tile([P, S], U8, name="gs", align_bytes=64)
-        gw = tiles("gw", PASSES, [P, S], U32)
+        gw0 = keep.tile([P, S], U32, name="gw0", align_bytes=64)
+        gw1 = tiles("gw1", 2, [P, S // 2], U32)
         nc.vector.tensor_copy(gs[:], xs[:].indirect(offs_sb[:]))
-        for o in range(PASSES):
-            nc.vector.tensor_copy(gw[o][:], xw[o][:].indirect(offs_sb[:]))
+        nc.vector.tensor_copy(gw0[:], xw[0][:].indirect(offs_sb[:]))
 
         w1_bf = tiles("w1_bf", PASSES, [P, H * PACK], BF16)
         w1_codes = tiles("w1_codes", PASSES, [P, H], U32)
         w1_sc = tiles("w1_sc", PASSES, [P, H], U8)
         ybank = [psum.tile([P, S], F32, name="ybank%d" % t) for t in range(PACK)]
         for o in range(PASSES):
-            dst = w1_bf[o][:].rearrange("p (t m j) -> p m t j", t=PACK, j=PACK)
-            for h, (lo, hi) in enumerate(W1_CHUNKS[o]):
-                nc.vector.tensor_copy(
-                    dst[:, lo // PACK : hi // PACK, :, :],
-                    w1_raw[o][h][:].rearrange("p j (m t) -> p m t j", t=PACK),
-                )
-            for lo, hi in ((0, H),) if o == 0 else ((0, 128), (128, 256), (256, 512)):
-                nc.vector.quantize_mx(
-                    out=w1_codes[o][:, lo:hi].bitcast(FP8X4), scales=w1_sc[o][:, lo:hi], in_=w1_bf[o][:, PACK * lo : PACK * hi]
-                )
-            for t in range(PACK):
-                cols = slice(P * t, P * (t + 1))
-                nc.tensor.matmul_mx(
-                    out=ybank[t][:],
-                    lhsT=w1_codes[o][:, cols].bitcast(FP8X4),
-                    lhsT_scale=w1_sc[o][:, cols],
-                    rhs=gw[o][:].bitcast(FP8X4),
-                    rhs_scale=gs[4 * o :, :],
-                    start=(o == 0),
-                    stop=(o == PASSES - 1),
-                )
+            nc.vector.tensor_copy(
+                w1_bf[o][:].rearrange("p (t m j) -> p m t j", t=PACK, j=PACK),
+                w1_raw[o][:].rearrange("p j (m t) -> p m t j", t=PACK),
+            )
+            nc.vector.quantize_mx(out=w1_codes[o][:].bitcast(FP8X4), scales=w1_sc[o][:], in_=w1_bf[o][:])
 
-        rden_t = keep.tile([P, PACK * S], F32, name="rden_t", tag="w1_bf1", align_bytes=64)
+        def product(t, o, words, weeks, start, stop):
+            cols = slice(P * t, P * (t + 1))
+            nc.tensor.matmul_mx(
+                out=ybank[t][:, weeks],
+                lhsT=w1_codes[o][:, cols].bitcast(FP8X4),
+                lhsT_scale=w1_sc[o][:, cols],
+                rhs=words[:].bitcast(FP8X4),
+                rhs_scale=gs[4 * o :, weeks],
+                start=start,
+                stop=stop,
+            )
+
+        for t in range(PACK):
+            product(t, 0, gw0, slice(0, S), True, False)
+        for h in range(2):
+            nc.vector.tensor_copy(gw1[h][:], xw[1][:].indirect(offs_sb[:, 16 * h : 16 * (h + 1)]))
+            for t in range(PACK):
+                product(t, 1, gw1[h], slice(S // 2 * h, S // 2 * (h + 1)), False, h == 1)
+
+        rden_t = keep.tile([P, PACK * S], F32, name="rden_t", tag="xw1", align_bytes=64)
         rden = [psum.tile([P, S], F32, name="rden%d" % t, tag="aux%d" % t) for t in range(PACK)]
         for t in range(PACK):
             nc.scalar.activation(rden_t[:, t * S : (t + 1) * S], lden[t][:], ACT.Exp, scale=-1.0)
@@ -145,14 +147,14 @@ def tile_picked_yalmon_star_p_kernel(
         hid = keep.tile([P, PACK, V], F32, name="hid", align_bytes=64)
 
         def side(t):
-            return nc.vector if t == PACK - 1 else nc.gpsimd
+            return nc.gpsimd if t < 2 else nc.vector
 
         def numerator(t):
             y = ybank[t]
             nc.vector.tensor_tensor(shifted[t][:, 0, : S - 1], y[:, 1:], we1[t][:, : S - 1], ALU.mult)
             nc.vector.tensor_tensor(shifted[t][:, 1, : S - 2], y[:, 2:], we2[t][:, : S - 2], ALU.mult)
             nc.vector.tensor_tensor(part[t][:], y[:], shifted[t][:, 0, :], ALU.add)
-            nc.gpsimd.tensor_tensor(num[t][:], part[t][:], shifted[t][:, 1, :], ALU.add)
+            (nc.gpsimd if t < 3 else nc.vector).tensor_tensor(num[t][:], part[t][:], shifted[t][:, 1, :], ALU.add)
 
         def damping(t):
             nc.scalar.activation(ysq[t][:], ybank[t][:], ACT.Square)
@@ -170,7 +172,7 @@ def tile_picked_yalmon_star_p_kernel(
             for lo in range(0, V, width):
                 cols = slice(lo, lo + width)
                 entries = slice(lo // 16, (lo + width) // 16)
-                if t in ():
+                if t in (0,):
                     nc.scalar.activation(zq[t][:, cols], mid[t][:].indirect(qtr_sb[:, entries]), ACT.Copy)
                 else:
                     nc.vector.tensor_copy(zq[t][:, cols], mid[t][:].indirect(qtr_sb[:, entries]))

@@ -172,7 +172,7 @@ def tile_picked_yalmon_star_p_kernel(
             for lo in range(0, V, width):
                 cols = slice(lo, lo + width)
                 entries = slice(lo // 16, (lo + width) // 16)
-                if t in (0,):
+                if t in (0, 1, 2, 3):
                     nc.scalar.activation(zq[t][:, cols], mid[t][:].indirect(qtr_sb[:, entries]), ACT.Copy)
                 else:
                     nc.vector.tensor_copy(zq[t][:, cols], mid[t][:].indirect(qtr_sb[:, entries]))

@@ -19,6 +19,7 @@ ALU = mybir.AluOpType
 P = 128
 PACK = 4
 PASSES = K // (P * PACK)
+EARLY = 256
 W1_CHUNKS = (((0, 256), (256, 512)), ((0, 256), (256, 384), (384, 512)))
 VH = V // 2
 
@@ -55,16 +56,20 @@ def tile_picked_yalmon_star_p_kernel(
         nc.sync.dma_start(out=t_first[:], in_=t_rows[:, 0, :])
         nc.sync.dma_start(out=t_rest[:], in_=t_rows[:, 1:, :])
         nc.sync.dma_start(offs_sb[:], offs)
-        for q in range(4):
-            nc.sync.dma_start(
-                out=xs[32 * q : 32 * q + 4 * PASSES, :].bitcast(I32),
-                in_=x_scales[:, 4 * q : 4 * q + 4, :].bitcast(I32),
-            )
+
+        def load_scales(o):
+            for q in range(4):
+                first = 32 * q + 4 * o
+                nc.sync.dma_start(
+                    out=xs[first : first + 4, :].bitcast(I32), in_=x_scales[o, 4 * q : 4 * q + 4, :].bitcast(I32)
+                )
 
         def load_words(o):
             nc.sync.dma_start(out=xw[o][:].bitcast(I32), in_=x_words[o].rearrange("p n r -> p (n r)").bitcast(I32))
 
+        load_scales(0)
         load_words(0)
+        load_scales(1)
         for o in range(PASSES):
             nc.sync.dma_start(out=w1_raw[o][:], in_=w1[512 * o : 512 * (o + 1), :].rearrange("(p j) c -> p j c", j=PACK))
         load_words(1)
@@ -135,6 +140,17 @@ def tile_picked_yalmon_star_p_kernel(
             for b in range(S // P):
                 nc.tensor.transpose(rden[t][:, P * b : P * (b + 1)], rden_t[:, t * S + P * b : t * S + P * (b + 1)], ident[:])
 
+        w2_bf = keep.tile([P, N * PACK], BF16, name="w2_bf", align_bytes=64)
+        w2_codes = keep.tile([P, N], U32, name="w2_codes", align_bytes=64)
+        w2_sc = keep.tile([P, N], U8, name="w2_sc", align_bytes=64)
+        nc.gpsimd.tensor_scalar(
+            w2_bf[:].rearrange("p (c i j) -> p c j i", i=4, j=PACK),
+            w2_raw[:].rearrange("p j (c i) -> p c j i", i=4),
+            1.0,
+            0.0,
+            ALU.mult,
+            ALU.add,
+        )
         part = tiles("part", PACK, [P, S], F32)
         num = tiles("num", PACK, [P, S], F32)
         mid = tiles("mid", PACK, [P, S], F32)
@@ -156,28 +172,32 @@ def tile_picked_yalmon_star_p_kernel(
             nc.vector.tensor_tensor(part[t][:], y[:], shifted[t][:, 0, :], ALU.add)
             (nc.gpsimd if t < 3 else nc.vector).tensor_tensor(num[t][:], part[t][:], shifted[t][:, 1, :], ALU.add)
 
+        def pieces(t):
+            width = VH if t == PACK - 1 else V
+            return [(slice(lo, lo + width), slice(lo // 16, (lo + width) // 16)) for lo in range(0, V, width)]
+
         def damping(t):
             nc.scalar.activation(ysq[t][:], ybank[t][:], ACT.Square)
-            if t in ():
-                nc.vector.tensor_copy(sl[t][:], ysq[t][:].indirect(lag_sb[:]))
-            else:
-                nc.scalar.activation(sl[t][:], ysq[t][:].indirect(lag_sb[:]), ACT.Copy)
-            nc.scalar.activation(damp[t][:], sl[t][:], ACT.Exp, scale=-1.0)
+            for cols, entries in pieces(t):
+                if t in ():
+                    nc.vector.tensor_copy(sl[t][:, cols], ysq[t][:].indirect(lag_sb[:, entries]))
+                else:
+                    nc.scalar.activation(sl[t][:, cols], ysq[t][:].indirect(lag_sb[:, entries]), ACT.Copy)
+                nc.scalar.activation(damp[t][:, cols], sl[t][:, cols], ACT.Exp, scale=-1.0)
 
         def average(t):
             nc.vector.scalar_tensor_tensor(mid[t][:], num[t][:], unit_sb[:, t : t + 1], rden[t][:], ALU.mult, ALU.mult)
 
+        def growth(t):
+            if t in ():
+                nc.scalar.activation(zq[t][:], mid[t][:].indirect(qtr_sb[:]), ACT.Copy)
+            else:
+                nc.vector.tensor_copy(zq[t][:], mid[t][:].indirect(qtr_sb[:]))
+            nc.scalar.activation(zl[t][:], mid[t][:].indirect(lag_sb[:]), ACT.Copy, scale=-0.7)
+            side(t).tensor_tensor(gr[t][:], zl[t][:], zq[t][:], ALU.add)
+
         def hidden(t):
-            width = VH if t == PACK - 1 else V
-            for lo in range(0, V, width):
-                cols = slice(lo, lo + width)
-                entries = slice(lo // 16, (lo + width) // 16)
-                if t in (0, 1, 2, 3):
-                    nc.scalar.activation(zq[t][:, cols], mid[t][:].indirect(qtr_sb[:, entries]), ACT.Copy)
-                else:
-                    nc.vector.tensor_copy(zq[t][:, cols], mid[t][:].indirect(qtr_sb[:, entries]))
-                nc.scalar.activation(zl[t][:, cols], mid[t][:].indirect(lag_sb[:, entries]), ACT.Copy, scale=-0.7)
-                side(t).tensor_tensor(gr[t][:, cols], zl[t][:, cols], zq[t][:, cols], ALU.add)
+            for cols, entries in pieces(t):
                 side(t).tensor_tensor(hid[:, t, cols], gr[t][:, cols], damp[t][:, cols], ALU.mult)
 
         numerator(0)
@@ -186,24 +206,21 @@ def tile_picked_yalmon_star_p_kernel(
         average(0)
         average(1)
         damping(0)
+        growth(0)
         hidden(0)
         numerator(3)
         average(2)
         damping(1)
+        growth(1)
         hidden(1)
         average(3)
         damping(2)
+        growth(2)
         hidden(2)
+        growth(3)
         damping(3)
         hidden(3)
 
-        w2_bf = keep.tile([P, N * PACK], BF16, name="w2_bf", align_bytes=64)
-        w2_codes = keep.tile([P, N], U32, name="w2_codes", align_bytes=64)
-        w2_sc = keep.tile([P, N], U8, name="w2_sc", align_bytes=64)
-        nc.vector.tensor_copy(
-            w2_bf[:].rearrange("p (c i j) -> p c j i", i=4, j=PACK),
-            w2_raw[:].rearrange("p j (c i) -> p c j i", i=4),
-        )
         nc.vector.quantize_mx(out=w2_codes[:].bitcast(FP8X4), scales=w2_sc[:], in_=w2_bf[:])
 
         hid_bf = tiles("hid_bf", V // VH, [P, VH * PACK], BF16)
@@ -212,7 +229,8 @@ def tile_picked_yalmon_star_p_kernel(
         res = tiles("res", V // VH, [P, VH], F32)
         for h in range(V // VH):
             cols = slice(h * VH, (h + 1) * VH)
-            nc.vector.tensor_copy(
+            weave = nc.scalar.copy if h == 0 else nc.vector.tensor_copy
+            weave(
                 hid_bf[h][:].rearrange("p (c i t) -> p c t i", i=4, t=PACK),
                 hid[:, :, cols].rearrange("p t (c i) -> p c t i", i=4),
             )

from contextlib import ExitStack

import concourse.mybir as mybir
from concourse.masks import make_identity

K, T, S, N, H, V = 1024, 2048, 512, 128, 512, 256
FLOPS = 2 * K * H * S + 2 * H * N * V

F32 = mybir.dt.float32
BF16 = mybir.dt.bfloat16
I32 = mybir.dt.int32
U32 = mybir.dt.uint32
U16 = mybir.dt.uint16
U8 = mybir.dt.uint8
FP8X4 = mybir.dt.float8_e4m3fn_x4
ACT = mybir.ActivationFunctionType
ALU = mybir.AluOpType

P = 128
PACK = 4
PASSES = K // (P * PACK)
EARLY = 256
W1_CHUNKS = (((0, 256), (256, 512)), ((0, 256), (256, 384), (384, 512)))
VH = V // 2


def tile_picked_yalmon_star_p_kernel(
    tc, x_words, x_scales, w1, t1, unit, w2, offs, qtr, lag, out
):
    nc = tc.nc
    with ExitStack() as ctx:
        keep = ctx.enter_context(tc.tile_pool(name="keep", bufs=1))
        psum = ctx.enter_context(tc.psum_pool(name="psum", bufs=1))

        def tiles(name, count, shape, dtype):
            return [keep.tile(shape, dtype, name="%s%d" % (name, i), tag="%s%d" % (name, i), align_bytes=64) for i in range(count)]

        offs_sb = keep.tile([P, S // 16], U16, name="offs_sb")
        qtr_sb = keep.tile([P, V // 16], U16, name="qtr_sb")
        lag_sb = keep.tile([P, V // 16], U16, name="lag_sb")
        unit_sb = keep.tile([P, PACK], F32, name="unit_sb")
        t_first = keep.tile([P, S], F32, name="t_first", align_bytes=64)
        t_rest = keep.tile([P, PACK - 1, S], F32, name="t_rest", align_bytes=64)
        t_sb = [t_first[:]] + [t_rest[:, t, :] for t in range(PACK - 1)]
        xw = tiles("xw", PASSES, [P, T], U32)
        xs = keep.tile([P, T], U8, name="xs", align_bytes=64)
        w1_raw = tiles("w1_raw", PASSES, [P, PACK, H], F32)
        w2_raw = keep.tile([P, PACK, N], F32, name="w2_raw", align_bytes=64)

        nc.vector.memset(xs[:].bitcast(I32), 0)
        shifted = tiles("shifted", PACK, [P, 2, S], F32)
        for t in range(PACK):
            nc.vector.memset(shifted[t][:, :, S - 2 :], 0.0)

        t_rows = t1.rearrange("(p t) c -> p t c", t=PACK)
        nc.sync.dma_start(out=t_first[:], in_=t_rows[:, 0, :])
        nc.sync.dma_start(out=t_rest[:], in_=t_rows[:, 1:, :])
        nc.sync.dma_start(offs_sb[:], offs)

        def load_scales(o):
            for q in range(4):
                first = 32 * q + 4 * o
                nc.sync.dma_start(
                    out=xs[first : first + 4, :].bitcast(I32), in_=x_scales[o, 4 * q : 4 * q + 4, :].bitcast(I32)
                )

        def load_words(o):
            nc.sync.dma_start(out=xw[o][:].bitcast(I32), in_=x_words[o].rearrange("p n r -> p (n r)").bitcast(I32))

        load_scales(0)
        load_words(0)
        load_scales(1)
        for o in range(PASSES):
            nc.sync.dma_start(out=w1_raw[o][:], in_=w1[512 * o : 512 * (o + 1), :].rearrange("(p j) c -> p j c", j=PACK))
        load_words(1)
        nc.sync.dma_start(out=unit_sb[:], in_=unit.rearrange("(p t) o -> p (t o)", t=PACK))
        nc.sync.dma_start(qtr_sb[:], qtr)
        nc.sync.dma_start(lag_sb[:], lag)
        nc.sync.dma_start(out=w2_raw[:], in_=w2.rearrange("(p j) c -> p j c", j=PACK))

        th1 = tiles("th1", PACK, [P, S], F32)
        th2 = tiles("th2", PACK, [P, S], F32)
        we1 = tiles("we1", PACK, [P, S], F32)
        we2 = tiles("we2", PACK, [P, S], F32)
        ident = keep.tile([P, P], F32, name="ident", align_bytes=64)
        make_identity(nc, ident[:])
        lden = tiles("lden", PACK, [P, S], F32)
        wsum = [psum.tile([P, S], F32, name="wsum%d" % t, tag="aux%d" % t) for t in range(PACK)]
        for t in range(PACK):
            nc.scalar.activation(th1[t][:], t_sb[t], ACT.Tanh)
            nc.scalar.activation(th2[t][:], t_sb[t], ACT.Tanh, scale=1.7)
            nc.scalar.activation(we1[t][:], th1[t][:], ACT.Exp, scale=0.8)
            nc.scalar.activation(we2[t][:], th2[t][:], ACT.Exp, scale=-0.8)
            for b in range(S // P):
                cols = slice(P * b, P * (b + 1))
                nc.tensor.matmul(wsum[t][:, cols], lhsT=we1[t][:, cols], rhs=ident[:], is_transpose=True, start=True, stop=False)
                nc.tensor.matmul(wsum[t][:, cols], lhsT=we2[t][:, cols], rhs=ident[:], is_transpose=True, start=False, stop=True)
        for t in range(PACK):
            nc.scalar.activation(lden[t][:], wsum[t][:], ACT.Ln, bias=1.0)
        gs = keep.tile([P, S], U8, name="gs", align_bytes=64)
        gw0 = keep.tile([P, S], U32, name="gw0", align_bytes=64)
        gw1 = tiles("gw1", 2, [P, S // 2], U32)
        nc.vector.tensor_copy(gs[:], xs[:].indirect(offs_sb[:]))
        nc.vector.tensor_copy(gw0[:], xw[0][:].indirect(offs_sb[:]))

        w1_bf = tiles("w1_bf", PASSES, [P, H * PACK], BF16)
        w1_codes = tiles("w1_codes", PASSES, [P, H], U32)
        w1_sc = tiles("w1_sc", PASSES, [P, H], U8)
        ybank = [psum.tile([P, S], F32, name="ybank%d" % t) for t in range(PACK)]
        for o in range(PASSES):
            nc.vector.tensor_copy(
                w1_bf[o][:].rearrange("p (t m j) -> p m t j", t=PACK, j=PACK),
                w1_raw[o][:].rearrange("p j (m t) -> p m t j", t=PACK),
            )
            nc.vector.quantize_mx(out=w1_codes[o][:].bitcast(FP8X4), scales=w1_sc[o][:], in_=w1_bf[o][:])

        def product(t, o, words, weeks, start, stop):
            cols = slice(P * t, P * (t + 1))
            nc.tensor.matmul_mx(
                out=ybank[t][:, weeks],
                lhsT=w1_codes[o][:, cols].bitcast(FP8X4),
                lhsT_scale=w1_sc[o][:, cols],
                rhs=words[:].bitcast(FP8X4),
                rhs_scale=gs[4 * o :, weeks],
                start=start,
                stop=stop,
            )

        for t in range(PACK):
            product(t, 0, gw0, slice(0, S), True, False)
        for h in range(2):
            nc.vector.tensor_copy(gw1[h][:], xw[1][:].indirect(offs_sb[:, 16 * h : 16 * (h + 1)]))
            for t in range(PACK):
                product(t, 1, gw1[h], slice(S // 2 * h, S // 2 * (h + 1)), False, h == 1)

        rden_t = keep.tile([P, PACK * S], F32, name="rden_t", tag="xw1", align_bytes=64)
        rden = [psum.tile([P, S], F32, name="rden%d" % t, tag="aux%d" % t) for t in range(PACK)]
        for t in range(PACK):
            nc.scalar.activation(rden_t[:, t * S : (t + 1) * S], lden[t][:], ACT.Exp, scale=-1.0)
            for b in range(S // P):
                nc.tensor.transpose(rden[t][:, P * b : P * (b + 1)], rden_t[:, t * S + P * b : t * S + P * (b + 1)], ident[:])

        w2_bf = keep.tile([P, N * PACK], BF16, name="w2_bf", align_bytes=64)
        w2_codes = keep.tile([P, N], U32, name="w2_codes", align_bytes=64)
        w2_sc = keep.tile([P, N], U8, name="w2_sc", align_bytes=64)
        nc.gpsimd.tensor_scalar(
            w2_bf[:].rearrange("p (c i j) -> p c j i", i=4, j=PACK),
            w2_raw[:].rearrange("p j (c i) -> p c j i", i=4),
            1.0,
            0.0,
            ALU.mult,
            ALU.add,
        )
        part = tiles("part", PACK, [P, S], F32)
        num = tiles("num", PACK, [P, S], F32)
        mid = tiles("mid", PACK, [P, S], F32)
        ysq = tiles("ysq", PACK, [P, S], F32)
        zq = tiles("zq", PACK, [P, V], F32)
        zl = tiles("zl", PACK, [P, V], F32)
        sl = tiles("sl", PACK, [P, V], F32)
        damp = tiles("damp", PACK, [P, V], F32)
        gr = tiles("gr", PACK, [P, V], F32)
        hid = keep.tile([P, PACK, V], F32, name="hid", align_bytes=64)

        def side(t):
            return nc.gpsimd if t < 2 else nc.vector

        def numerator(t):
            y = ybank[t]
            nc.vector.tensor_tensor(shifted[t][:, 0, : S - 1], y[:, 1:], we1[t][:, : S - 1], ALU.mult)
            nc.vector.tensor_tensor(shifted[t][:, 1, : S - 2], y[:, 2:], we2[t][:, : S - 2], ALU.mult)
            nc.vector.tensor_tensor(part[t][:], y[:], shifted[t][:, 0, :], ALU.add)
            (nc.gpsimd if t < 3 else nc.vector).tensor_tensor(num[t][:], part[t][:], shifted[t][:, 1, :], ALU.add)

        def pieces(t):
            width = VH if t == PACK - 1 else V
            return [(slice(lo, lo + width), slice(lo // 16, (lo + width) // 16)) for lo in range(0, V, width)]

        def damping(t):
            nc.scalar.activation(ysq[t][:], ybank[t][:], ACT.Square)
            for cols, entries in pieces(t):
                if t in ():
                    nc.vector.tensor_copy(sl[t][:, cols], ysq[t][:].indirect(lag_sb[:, entries]))
                else:
                    nc.scalar.activation(sl[t][:, cols], ysq[t][:].indirect(lag_sb[:, entries]), ACT.Copy)
                nc.scalar.activation(damp[t][:, cols], sl[t][:, cols], ACT.Exp, scale=-1.0)

        def average(t):
            nc.vector.scalar_tensor_tensor(mid[t][:], num[t][:], unit_sb[:, t : t + 1], rden[t][:], ALU.mult, ALU.mult)

        def growth(t):
            if t in ():
                nc.scalar.activation(zq[t][:], mid[t][:].indirect(qtr_sb[:]), ACT.Copy)
            else:
                nc.vector.tensor_copy(zq[t][:], mid[t][:].indirect(qtr_sb[:]))
            nc.scalar.activation(zl[t][:], mid[t][:].indirect(lag_sb[:]), ACT.Copy, scale=-0.7)
            side(t).tensor_tensor(gr[t][:], zl[t][:], zq[t][:], ALU.add)

        def hidden(t):
            for cols, entries in pieces(t):
                side(t).tensor_tensor(hid[:, t, cols], gr[t][:, cols], damp[t][:, cols], ALU.mult)

        numerator(0)
        numerator(1)
        numerator(2)
        average(0)
        average(1)
        damping(0)
        growth(0)
        hidden(0)
        numerator(3)
        average(2)
        damping(1)
        growth(1)
        hidden(1)
        average(3)
        damping(2)
        growth(2)
        hidden(2)
        growth(3)
        damping(3)
        hidden(3)

        nc.vector.quantize_mx(out=w2_codes[:].bitcast(FP8X4), scales=w2_sc[:], in_=w2_bf[:])

        hid_bf = tiles("hid_bf", V // VH, [P, VH * PACK], BF16)
        hid_codes = tiles("hid_codes", V // VH, [P, VH], U32)
        hid_sc = tiles("hid_sc", V // VH, [P, VH], U8)
        res = tiles("res", V // VH, [P, VH], F32)
        for h in range(V // VH):
            cols = slice(h * VH, (h + 1) * VH)
            weave = nc.scalar.copy if h == 0 else nc.vector.tensor_copy
            weave(
                hid_bf[h][:].rearrange("p (c i t) -> p c t i", i=4, t=PACK),
                hid[:, :, cols].rearrange("p t (c i) -> p c t i", i=4),
            )
            nc.vector.quantize_mx(out=hid_codes[h][:].bitcast(FP8X4), scales=hid_sc[h][:], in_=hid_bf[h][:])
            obank = psum.tile([P, VH], F32, name="obank%d" % h, tag="aux%d" % h)
            nc.tensor.matmul_mx(
                out=obank[:],
                lhsT=w2_codes[:].bitcast(FP8X4),
                lhsT_scale=w2_sc[:],
                rhs=hid_codes[h][:].bitcast(FP8X4),
                rhs_scale=hid_sc[h][:],
                start=True,
                stop=True,
            )
            nc.scalar.copy(res[h][:], obank[:])
            nc.sync.dma_start(out=out[:, cols], in_=res[h][:])
